import numpy as np
import ml_dtypes

BF16 = ml_dtypes.bfloat16


def bf(x):
    return np.asarray(x, np.float32).astype(BF16)


def f32(x):
    return np.asarray(x, np.float32)


def f64(x):
    return np.asarray(x).astype(np.float64)


def striped(idx):
    return np.tile(idx.reshape(-1, 16).T, (8, 1))


S, A, K, M, N, E, Q = 512, 512, 256, 256, 256, 4, 64


def setup_inputs():
    return {"x": bf(np.random.standard_normal((A, S))), "wd": bf(np.random.standard_normal((A, M)) / np.sqrt(A)), "y": bf(np.random.standard_normal((K, N))), "w": bf(np.random.standard_normal((E, K, M)) / np.sqrt(K)), "b": f32(0.5 * np.random.standard_normal((M, 1))), "offs": striped(np.random.permutation(S)[:N])}


def reference(x, wd, y, w, b, offs):
    idx = offs[:16].T.reshape(-1)
    z = f64(wd).T @ f64(x)
    for e in range(E):
        z[:, idx[e * Q : (e + 1) * Q]] += f64(w)[e].T @ f64(y)[:, e * Q : (e + 1) * Q]
    return np.tanh(z + f64(b))

@@ -1,0 +1,72 @@
+import concourse.mybir as mybir
+
+BF16, F32, U16 = mybir.dt.bfloat16, mybir.dt.float32, mybir.dt.uint16
+TANH = mybir.ActivationFunctionType.Tanh
+
+P = 128
+S = 512
+D = 512
+K = 256
+M = 256
+N = 256
+E = 4
+Q = N // E
+DB = D // P
+KB = K // P
+MB = M // P
+OC = Q // 16
+
+FLOPS = 2 * D * M * S + 2 * K * M * N
+
+
+def tile_rows_fillproj_tanh_kernel(tc, x, wd, y, w, b, offs, out):
+    nc = tc.nc
+    with (
+        tc.tile_pool(name="held", bufs=1) as held,
+        tc.psum_pool(name="psum", bufs=1) as psum,
+    ):
+        x_rows = x.rearrange("(p a) s -> p a s", a=DB)
+        half = DB // 2
+        wd_t = held.tile([P, DB, M], BF16, name="wd_t")
+        x_lo = held.tile([P, half, S], BF16, name="x_lo")
+        x_hi = held.tile([P, half, S], BF16, name="x_hi")
+        offsets = held.tile([P, N // 16], U16, name="offsets")
+        y_t = held.tile([P, KB, N], BF16, name="y_t")
+        w_t = held.tile([P, E, KB, M], BF16, name="w_t")
+        bias = held.tile([P, MB], F32, name="bias")
+
+        nc.sync.dma_start(wd_t[:], wd.rearrange("(p a) m -> p a m", a=DB))
+        nc.sync.dma_start(x_lo[:], x_rows[:, 0:half, :])
+        nc.sync.dma_start(x_hi[:], x_rows[:, half:DB, :])
+        nc.sync.dma_start(offsets[:], offs)
+        nc.sync.dma_start(y_t[:], y.rearrange("(p a) n -> p a n", a=KB))
+        nc.sync.dma_start(w_t[:], w.rearrange("e (p a) m -> p e a m", a=KB))
+        nc.sync.dma_start(bias[:], b.rearrange("(c p) o -> p (c o)", p=P))
+
+        windows = [psum.tile([P, S], F32, name=f"window{c}") for c in range(MB)]
+        for a in range(DB):
+            x_block = x_lo[:, a, :] if a < half else x_hi[:, a - half, :]
+            for c in range(MB):
+                nc.tensor.matmul(
+                    windows[c][:],
+                    wd_t[:, a, c * P : (c + 1) * P],
+                    x_block,
+                    start=(a == 0),
+                    stop=False,
+                )
+
+        for c in range(MB):
+            for e in range(E):
+                for a in range(KB):
+                    nc.tensor.matmul(
+                        windows[c][:].indirect(offsets[:, e * OC : (e + 1) * OC]),
+                        w_t[:, e, a, c * P : (c + 1) * P],
+                        y_t[:, a, e * Q : (e + 1) * Q],
+                        start=False,
+                        stop=(e == E - 1 and a == KB - 1),
+                    )
+
+        for c in range(MB):
+            result = held.tile([P, S], F32, name=f"result{c}")
+            nc.scalar.activation(result[:], windows[c][:], TANH, bias=bias[:, c : c + 1])
+            nc.sync.dma_start(out[c * P : (c + 1) * P, :], result[:])

@@ -15,6 +15,7 @@ DB = D // P
 KB = K // P
 MB = M // P
 OC = Q // 16
+WARMUPS = 5
 
 FLOPS = 2 * D * M * S + 2 * K * M * N
 
@@ -35,6 +36,11 @@ def tile_rows_fillproj_tanh_kernel(tc, x, wd, y, w, b, offs, out):
         w_t = held.tile([P, E, KB, M], BF16, name="w_t")
         bias = held.tile([P, MB], F32, name="bias")
 
+        zeros = held.tile([P, S], BF16, name="zeros")
+        tanh_sink = held.tile([P, 1], F32, name="tanh_sink")
+        matmul_sink = psum.tile([P, S], F32, name="matmul_sink")
+        nc.vector.memset(zeros[:], 0.0)
+
         nc.sync.dma_start(wd_t[:], wd.rearrange("(p a) m -> p a m", a=DB))
         nc.sync.dma_start(x_lo[:], x_rows[:, 0:half, :])
         nc.sync.dma_start(x_hi[:], x_rows[:, half:DB, :])
@@ -42,6 +48,10 @@ def tile_rows_fillproj_tanh_kernel(tc, x, wd, y, w, b, offs, out):
         nc.sync.dma_start(y_t[:], y.rearrange("(p a) n -> p a n", a=KB))
         nc.sync.dma_start(w_t[:], w.rearrange("e (p a) m -> p e a m", a=KB))
         nc.sync.dma_start(bias[:], b.rearrange("(c p) o -> p (c o)", p=P))
+
+        nc.scalar.activation(tanh_sink[:], zeros[:, 0:1], TANH)
+        for i in range(WARMUPS):
+            nc.tensor.matmul(matmul_sink[:], zeros[:, 0:P], zeros[:], start=True, stop=True)
 
         windows = [psum.tile([P, S], F32, name=f"window{c}") for c in range(MB)]
         for a in range(DB):

@@ -15,7 +15,9 @@ DB = D // P
 KB = K // P
 MB = M // P
 OC = Q // 16
-WARMUPS = 5
+HB = DB // 2
+HE = E // 2
+WARMUPS = 14
 
 FLOPS = 2 * D * M * S + 2 * K * M * N
 
@@ -27,40 +29,40 @@ def tile_rows_fillproj_tanh_kernel(tc, x, wd, y, w, b, offs, out):
         tc.psum_pool(name="psum", bufs=1) as psum,
     ):
         x_rows = x.rearrange("(p a) s -> p a s", a=DB)
-        half = DB // 2
-        wd_t = held.tile([P, DB, M], BF16, name="wd_t")
-        x_lo = held.tile([P, half, S], BF16, name="x_lo")
-        x_hi = held.tile([P, half, S], BF16, name="x_hi")
+        wd_rows = wd.rearrange("(p a) m -> p a m", a=DB)
+        w_rows = w.rearrange("e (p a) m -> p e a m", a=KB)
+        wd_t = [held.tile([P, HB, M], BF16, name=f"wd{h}") for h in range(2)]
+        x_t = [held.tile([P, HB, S], BF16, name=f"x{h}") for h in range(2)]
         offsets = held.tile([P, N // 16], U16, name="offsets")
         y_t = held.tile([P, KB, N], BF16, name="y_t")
-        w_t = held.tile([P, E, KB, M], BF16, name="w_t")
+        w_t = [held.tile([P, HE, KB, M], BF16, name=f"w{h}") for h in range(2)]
         bias = held.tile([P, MB], F32, name="bias")
 
-        zeros = held.tile([P, S], BF16, name="zeros")
+        zeros = held.tile([P, P], BF16, name="zeros")
         tanh_sink = held.tile([P, 1], F32, name="tanh_sink")
-        matmul_sink = psum.tile([P, S], F32, name="matmul_sink")
+        matmul_sink = psum.tile([P, P], F32, name="matmul_sink")
         nc.vector.memset(zeros[:], 0.0)
 
-        nc.sync.dma_start(wd_t[:], wd.rearrange("(p a) m -> p a m", a=DB))
-        nc.sync.dma_start(x_lo[:], x_rows[:, 0:half, :])
-        nc.sync.dma_start(x_hi[:], x_rows[:, half:DB, :])
+        for h in range(2):
+            nc.sync.dma_start(wd_t[h][:], wd_rows[:, h * HB : (h + 1) * HB, :])
+            nc.sync.dma_start(x_t[h][:], x_rows[:, h * HB : (h + 1) * HB, :])
         nc.sync.dma_start(offsets[:], offs)
         nc.sync.dma_start(y_t[:], y.rearrange("(p a) n -> p a n", a=KB))
-        nc.sync.dma_start(w_t[:], w.rearrange("e (p a) m -> p e a m", a=KB))
+        for h in range(2):
+            nc.sync.dma_start(w_t[h][:], w_rows[:, h * HE : (h + 1) * HE, :, :])
         nc.sync.dma_start(bias[:], b.rearrange("(c p) o -> p (c o)", p=P))
 
         nc.scalar.activation(tanh_sink[:], zeros[:, 0:1], TANH)
         for i in range(WARMUPS):
-            nc.tensor.matmul(matmul_sink[:], zeros[:, 0:P], zeros[:], start=True, stop=True)
+            nc.tensor.matmul(matmul_sink[:], zeros[:], zeros[:], start=True, stop=True)
 
         windows = [psum.tile([P, S], F32, name=f"window{c}") for c in range(MB)]
         for a in range(DB):
-            x_block = x_lo[:, a, :] if a < half else x_hi[:, a - half, :]
             for c in range(MB):
                 nc.tensor.matmul(
                     windows[c][:],
-                    wd_t[:, a, c * P : (c + 1) * P],
-                    x_block,
+                    wd_t[a // HB][:, a % HB, c * P : (c + 1) * P],
+                    x_t[a // HB][:, a % HB, :],
                     start=(a == 0),
                     stop=False,
                 )
@@ -70,7 +72,7 @@ def tile_rows_fillproj_tanh_kernel(tc, x, wd, y, w, b, offs, out):
                 for a in range(KB):
                     nc.tensor.matmul(
                         windows[c][:].indirect(offsets[:, e * OC : (e + 1) * OC]),
-                        w_t[:, e, a, c * P : (c + 1) * P],
+                        w_t[e // HE][:, e % HE, a, c * P : (c + 1) * P],
                         y_t[:, a, e * Q : (e + 1) * Q],
                         start=False,
                         stop=(e == E - 1 and a == KB - 1),

@@ -17,7 +17,7 @@ MB = M // P
 OC = Q // 16
 HB = DB // 2
 HE = E // 2
-WARMUPS = 14
+WARMUPS = 12
 
 FLOPS = 2 * D * M * S + 2 * K * M * N
 
@@ -32,7 +32,7 @@ def tile_rows_fillproj_tanh_kernel(tc, x, wd, y, w, b, offs, out):
         wd_rows = wd.rearrange("(p a) m -> p a m", a=DB)
         w_rows = w.rearrange("e (p a) m -> p e a m", a=KB)
         wd_t = [held.tile([P, HB, M], BF16, name=f"wd{h}") for h in range(2)]
-        x_t = [held.tile([P, HB, S], BF16, name=f"x{h}") for h in range(2)]
+        x_t = [held.tile([P, S], BF16, name=f"x{a}") for a in range(DB)]
         offsets = held.tile([P, N // 16], U16, name="offsets")
         y_t = held.tile([P, KB, N], BF16, name="y_t")
         w_t = [held.tile([P, HE, KB, M], BF16, name=f"w{h}") for h in range(2)]
@@ -44,8 +44,9 @@ def tile_rows_fillproj_tanh_kernel(tc, x, wd, y, w, b, offs, out):
         nc.vector.memset(zeros[:], 0.0)
 
         for h in range(2):
-            nc.sync.dma_start(wd_t[h][:], wd_rows[:, h * HB : (h + 1) * HB, :])
-            nc.sync.dma_start(x_t[h][:], x_rows[:, h * HB : (h + 1) * HB, :])
+            nc.scalar.dma_start(wd_t[h][:], wd_rows[:, h * HB : (h + 1) * HB, :])
+        for a in range(DB):
+            nc.sync.dma_start(x_t[a][:], x_rows[:, a, :])
         nc.sync.dma_start(offsets[:], offs)
         nc.sync.dma_start(y_t[:], y.rearrange("(p a) n -> p a n", a=KB))
         for h in range(2):
@@ -62,7 +63,7 @@ def tile_rows_fillproj_tanh_kernel(tc, x, wd, y, w, b, offs, out):
                 nc.tensor.matmul(
                     windows[c][:],
                     wd_t[a // HB][:, a % HB, c * P : (c + 1) * P],
-                    x_t[a // HB][:, a % HB, :],
+                    x_t[a][:],
                     start=(a == 0),
                     stop=False,
                 )

import concourse.mybir as mybir

BF16, F32, U16 = mybir.dt.bfloat16, mybir.dt.float32, mybir.dt.uint16
TANH = mybir.ActivationFunctionType.Tanh

P = 128
S = 512
D = 512
K = 256
M = 256
N = 256
E = 4
Q = N // E
DB = D // P
KB = K // P
MB = M // P
OC = Q // 16
HB = DB // 2
HE = E // 2
WARMUPS = 12

FLOPS = 2 * D * M * S + 2 * K * M * N


def tile_rows_fillproj_tanh_kernel(tc, x, wd, y, w, b, offs, out):
    nc = tc.nc
    with (
        tc.tile_pool(name="held", bufs=1) as held,
        tc.psum_pool(name="psum", bufs=1) as psum,
    ):
        x_rows = x.rearrange("(p a) s -> p a s", a=DB)
        wd_rows = wd.rearrange("(p a) m -> p a m", a=DB)
        w_rows = w.rearrange("e (p a) m -> p e a m", a=KB)
        wd_t = [held.tile([P, HB, M], BF16, name=f"wd{h}") for h in range(2)]
        x_t = [held.tile([P, S], BF16, name=f"x{a}") for a in range(DB)]
        offsets = held.tile([P, N // 16], U16, name="offsets")
        y_t = held.tile([P, KB, N], BF16, name="y_t")
        w_t = [held.tile([P, HE, KB, M], BF16, name=f"w{h}") for h in range(2)]
        bias = held.tile([P, MB], F32, name="bias")

        zeros = held.tile([P, P], BF16, name="zeros")
        tanh_sink = held.tile([P, 1], F32, name="tanh_sink")
        matmul_sink = psum.tile([P, P], F32, name="matmul_sink")
        nc.vector.memset(zeros[:], 0.0)

        for h in range(2):
            nc.scalar.dma_start(wd_t[h][:], wd_rows[:, h * HB : (h + 1) * HB, :])
        for a in range(DB):
            nc.sync.dma_start(x_t[a][:], x_rows[:, a, :])
        nc.sync.dma_start(offsets[:], offs)
        nc.sync.dma_start(y_t[:], y.rearrange("(p a) n -> p a n", a=KB))
        for h in range(2):
            nc.sync.dma_start(w_t[h][:], w_rows[:, h * HE : (h + 1) * HE, :, :])
        nc.sync.dma_start(bias[:], b.rearrange("(c p) o -> p (c o)", p=P))

        nc.scalar.activation(tanh_sink[:], zeros[:, 0:1], TANH)
        for i in range(WARMUPS):
            nc.tensor.matmul(matmul_sink[:], zeros[:], zeros[:], start=True, stop=True)

        windows = [psum.tile([P, S], F32, name=f"window{c}") for c in range(MB)]
        for a in range(DB):
            for c in range(MB):
                nc.tensor.matmul(
                    windows[c][:],
                    wd_t[a // HB][:, a % HB, c * P : (c + 1) * P],
                    x_t[a][:],
                    start=(a == 0),
                    stop=False,
                )

        for c in range(MB):
            for e in range(E):
                for a in range(KB):
                    nc.tensor.matmul(
                        windows[c][:].indirect(offsets[:, e * OC : (e + 1) * OC]),
                        w_t[e // HE][:, e % HE, a, c * P : (c + 1) * P],
                        y_t[:, a, e * Q : (e + 1) * Q],
                        start=False,
                        stop=(e == E - 1 and a == KB - 1),
                    )

        for c in range(MB):
            result = held.tile([P, S], F32, name=f"result{c}")
            nc.scalar.activation(result[:], windows[c][:], TANH, bias=bias[:, c : c + 1])
            nc.sync.dma_start(out[c * P : (c + 1) * P, :], result[:])
